import numpy as np
import ml_dtypes


def mxq(x, axis, fmt="e4m3"):
    dtype, down = {"e4m3": (ml_dtypes.float8_e4m3fn, 7), "e5m2": (ml_dtypes.float8_e5m2, 14)}[fmt]
    v = np.moveaxis(np.asarray(x, np.float32).astype(ml_dtypes.bfloat16).astype(np.float64), axis, -1)
    blocks = v.reshape(v.shape[:-1] + (-1, 32))
    amax = np.abs(blocks).max(-1, keepdims=True)
    byte = np.maximum(np.where(amax > 0, np.frexp(amax)[1] - 1 + 127, 0) - down, 1)
    scale = np.exp2(byte - 127.0)
    codes = (blocks / scale).astype(np.float32).astype(dtype).astype(np.float64)
    return np.moveaxis((codes * scale).reshape(v.shape), -1, axis)


WIDE = False


def mx_kscale(k):
    if not WIDE:
        return np.ones(k)
    levels = np.array([10, -10, 5, -5, 0])
    if k % 512:
        return np.exp2(np.random.permutation(np.resize(levels, k // 32))).repeat(32)
    a = np.empty((k // 512, 16))
    for p in range(k // 512):
        a[p, :8] = np.random.permutation(np.resize(levels, 8))
        for g in range(8):
            far = levels[np.abs(levels - a[p, g]) >= 10]
            a[p, g + 8] = far[np.random.randint(len(far))]
    return np.exp2(a.ravel()).repeat(32)


def f64(x):
    return np.asarray(x).astype(np.float64)


def striped(idx):
    return np.tile(np.asarray(idx).reshape(-1, 16).T, (8, 1)).astype(np.uint16)


def unstriped(offs):
    return offs[:16].T.reshape(-1).astype(np.int64)


def striped8(idx):
    return np.asarray(idx).reshape(8, -1, 16).transpose(0, 2, 1).reshape(128, -1).astype(np.uint16)


def unstriped8(offs):
    return offs.reshape(8, 16, -1).transpose(0, 2, 1).reshape(8, -1).astype(np.int64)


def pick8(x, idx, run):
    r = np.arange(len(x))
    return x[r[:, None], idx[r % (8 * run) // run]]


E2M1 = np.array([0.0, 0.5, 1.0, 1.5, 2.0, 3.0, 4.0, 6.0, -0.0, -0.5, -1.0, -1.5, -2.0, -3.0, -4.0, -6.0])


def pack_weight(w, fmt):
    k, n = w.shape
    w = f64(np.asarray(w, np.float32).astype(ml_dtypes.bfloat16)).reshape(k // 32, 32, n)
    amax = np.abs(w).max(1)
    if fmt == "e4m3":
        byte = np.frexp(amax)[1] - 1 + 127 - 7
    else:
        mant, ex = np.frexp(amax / 6.0)
        byte = np.where(mant > 0.5, ex, ex - 1) + 127
    byte = np.clip(np.where(amax > 0, byte, 1), 1, 254)
    scaled = (w * np.exp2(127.0 - byte)[:, None, :]).reshape(k, n).astype(np.float32)
    by_word = np.ascontiguousarray(scaled.reshape(k // 512, 128, 4, n).transpose(0, 1, 3, 2))
    if fmt == "e4m3":
        words = by_word.astype(ml_dtypes.float8_e4m3fn).view(np.uint8)
    else:
        c = by_word.astype(ml_dtypes.float4_e2m1fn).view(np.uint8) & 0xF
        words = (c[..., 0::2] | (c[..., 1::2] << 4)).reshape(k // 512, 128, 2 * n)
    return np.ascontiguousarray(words), np.ascontiguousarray(byte.astype(np.uint8).reshape(k // 512, 16, n))


def unpack_weight(words, scales, fmt):
    g, _, n = scales.shape
    words = np.ascontiguousarray(words).reshape(g, 128, n, -1)
    if fmt == "e4m3":
        vals = words.view(ml_dtypes.float8_e4m3fn).astype(np.float64)
    else:
        nib = np.empty((g, 128, n, 4), np.uint8)
        nib[..., 0::2] = words & 0xF
        nib[..., 1::2] = words >> 4
        vals = E2M1[nib]
    vals = vals * np.repeat(np.exp2(scales.astype(np.float64) - 127.0), 8, axis=1)[..., None]
    return vals.transpose(0, 1, 3, 2).reshape(g * 512, n)


def sgn(shape):
    return np.random.uniform(0.5, 2.0, shape) * np.where(np.random.standard_normal(shape) < 0, -1.0, 1.0)


K, J, R, T, F, S, O, N, U = 512, 1024, 512, 2048, 1024, 512, 256, 256, 128


def setup_inputs():
    n = np.random.standard_normal
    idx = np.random.permutation(T)[:J]
    idx2 = np.stack([np.random.permutation(F)[:R] for _ in range(8)])
    idx3 = np.stack([np.random.permutation(J)[:S] for _ in range(8)])
    idx4 = np.random.permutation(J)[:S]
    idx5 = np.random.permutation(T)[:O]
    idx6 = np.stack([np.random.permutation(O)[:U] for _ in range(8)])
    idx7 = np.stack([np.random.permutation(O)[:U] for _ in range(8)])
    fk = mx_kscale(K)
    fr = mx_kscale(R)
    xtp = pack_weight(n((K, T)) * fk[:, None], "e4m3")
    wbp = pack_weight(n((R, N)) * 1 / np.sqrt(R) / fr[:, None], "e2m1")
    wsp = pack_weight(n((K, N)) * 1 / np.sqrt(K) / fk[:, None], "e2m1")
    return {
        "xt_words": xtp[0],
        "xt_scales": xtp[1],
        "ua": (np.random.randint(-7, 8, (K, F)).astype(np.float64)).astype(np.float32),
        "ha": ((np.random.randint(8, 25, (K, 1)) / 1024.0) / fk[:, None]).astype(np.float32),
        "sa": (sgn((R, 1)) * fr[:, None]).astype(np.float32),
        "sb": (sgn((R, 1)) * fr[:, None]).astype(np.float32),
        "wb_words": wbp[0],
        "wb_scales": wbp[1],
        "ws_words": wsp[0],
        "ws_scales": wsp[1],
        "so": (np.random.uniform(0.5, 1.6, (N, 1))).astype(np.float32),
        "sp": (np.random.uniform(0.5, 1.6, (N, 1))).astype(np.float32),
        "offs": striped(idx),
        "offs2": striped8(idx2),
        "offs3": striped8(idx3),
        "offs4": striped(idx4),
        "offs5": striped(idx5),
        "offs6": striped8(idx6),
        "offs7": striped8(idx7),
    }


def reference(xt_words, xt_scales, ua, ha, sa, sb, wb_words, wb_scales, ws_words, ws_scales, so, sp, offs, offs2, offs3, offs4, offs5, offs6, offs7):
    idx = unstriped(offs)
    idx2 = unstriped8(offs2)
    idx3 = unstriped8(offs3)
    idx4 = unstriped(offs4)
    idx5 = unstriped(offs5)
    idx6 = unstriped8(offs6)
    idx7 = unstriped8(offs7)
    xtu = unpack_weight(xt_words, xt_scales, "e4m3")
    wbu = unpack_weight(wb_words, wb_scales, "e2m1")
    wsu = unpack_weight(ws_words, ws_scales, "e2m1")
    wc = pick8(f64(ua), idx2, 64) * f64(ha)
    wcq = mxq(wc, 0, "e4m3")
    xtidxg = xtu[:, idx]
    a = wcq.T @ xtidxg
    h1 = np.maximum(pick8(a, idx3, 64) * f64(sa), a[:, idx4] * f64(sb))
    hid = h1.reshape(R, O, S // O).max(axis=2)
    hidq = mxq(hid, 0, "e4m3")
    xtidx5g = xtu[:, idx5]
    p = wbu.T @ hidq + wsu.T @ xtidx5g
    y = np.maximum(pick8(p, idx6, 16) * f64(so), pick8(p, idx7, 16) * f64(sp))
    return y

@@ -1,0 +1,191 @@
+from contextlib import ExitStack
+
+import concourse.mybir as mybir
+
+K, J, R, T, F, S, O, N, U = 512, 1024, 512, 2048, 1024, 512, 256, 256, 128
+FLOPS = 2 * K * R * J + 2 * R * N * O + 2 * K * N * O
+
+F32 = mybir.dt.float32
+BF16 = mybir.dt.bfloat16
+I32 = mybir.dt.int32
+U32 = mybir.dt.uint32
+U16 = mybir.dt.uint16
+U8 = mybir.dt.uint8
+FP8X4 = mybir.dt.float8_e4m3fn_x4
+FP4X4 = mybir.dt.float4_e2m1fn_x4
+COPY = mybir.ActivationFunctionType.Copy
+MAX = mybir.AluOpType.max
+XY = mybir.AxisListType.XY
+
+P = 128
+PACK = 4
+PER_COL = 16
+BANK = 512
+HALF_O = O // 2
+
+
+def tile_picked_tokens_codes_one_pooledgroups_further_grouppairs_kernel(
+    tc, xt_words, xt_scales, ua, ha, sa, sb, wb_words, wb_scales, ws_words, ws_scales, so, sp,
+    offs, offs2, offs3, offs4, offs5, offs6, offs7, out,
+):
+    nc = tc.nc
+    with ExitStack() as ctx:
+        keep = ctx.enter_context(tc.tile_pool(name="keep", bufs=1))
+        psum = ctx.enter_context(tc.psum_pool(name="psum", bufs=1))
+
+        def load_list(src, name):
+            t = keep.tile(list(src.shape), U16, name=name)
+            nc.sync.dma_start(t[:], src)
+            return t
+
+        def load_scale_rows(dst, src, queue):
+            for q in range(4):
+                queue.dma_start(dst[32 * q : 32 * q + 4, :].bitcast(I32), src[0, 4 * q : 4 * q + 4, :].bitcast(I32))
+
+        def part(lst, start, n):
+            return lst[:, start // PER_COL : (start + n) // PER_COL]
+
+        xs_win = keep.tile([P, T], U8, name="xs_win", align_bytes=64)
+        nc.vector.memset(xs_win[:].bitcast(I32), 0)
+        ua_rows = ua.rearrange("(p t) f -> t p f", t=PACK)
+        ua_win = [keep.tile([P, F], F32, name=f"ua_win{t}") for t in range(PACK)]
+        l2 = load_list(offs2, "l2")
+        l1 = load_list(offs, "l1")
+        nc.scalar.dma_start(ua_win[0][:], ua_rows[0])
+        nc.scalar.dma_start(ua_win[1][:], ua_rows[1])
+        ha_t = keep.tile([P, PACK], F32, name="ha_t")
+        nc.gpsimd.dma_start(ha_t[:], ha.rearrange("(p t) o -> p (t o)", t=PACK))
+        load_scale_rows(xs_win, xt_scales, nc.sync)
+        nc.sync.dma_start(ua_win[2][:], ua_rows[2])
+        nc.sync.dma_start(ua_win[3][:], ua_rows[3])
+        l5 = load_list(offs5, "l5")
+        xw_win = keep.tile([P, T], U32, name="xw_win", align_bytes=64)
+        nc.sync.dma_start(xw_win[:].bitcast(I32), xt_words[0].rearrange("p n t -> p (n t)").bitcast(I32))
+        l3 = load_list(offs3, "l3")
+        l4 = load_list(offs4, "l4")
+        sa_t = keep.tile([P, PACK], F32, name="sa_t")
+        nc.sync.dma_start(sa_t[:], sa.rearrange("(p t) o -> p (t o)", t=PACK))
+        sb_t = keep.tile([P, PACK], F32, name="sb_t")
+        nc.sync.dma_start(sb_t[:], sb.rearrange("(p t) o -> p (t o)", t=PACK))
+
+        ws_w = keep.tile([P, 2 * N], U8, name="ws_w", align_bytes=64)
+        wb_w = keep.tile([P, 2 * N], U8, name="wb_w", align_bytes=64)
+        ws_s = keep.tile([P, N], U8, name="ws_s", align_bytes=64)
+        wb_s = keep.tile([P, N], U8, name="wb_s", align_bytes=64)
+        nc.gpsimd.memset(ws_s[:].bitcast(I32), 0)
+        nc.gpsimd.memset(wb_s[:].bitcast(I32), 0)
+        nc.sync.dma_start(ws_w[:].bitcast(I32), ws_words[0].bitcast(I32))
+        load_scale_rows(ws_s, ws_scales, nc.sync)
+        nc.sync.dma_start(wb_w[:].bitcast(I32), wb_words[0].bitcast(I32))
+        load_scale_rows(wb_s, wb_scales, nc.sync)
+        l6 = load_list(offs6, "l6")
+        l7 = load_list(offs7, "l7")
+        so_t = keep.tile([P, 2], F32, name="so_t")
+        sp_t = keep.tile([P, 2], F32, name="sp_t")
+        with nc.allow_non_contiguous_dma(reason="one value a partition and output tile"):
+            nc.sync.dma_start(so_t[:], so.rearrange("(u p) o -> p (u o)", p=P))
+            nc.sync.dma_start(sp_t[:], sp.rearrange("(u p) o -> p (u o)", p=P))
+
+        xs_g = [keep.tile([P, BANK], U8, name=f"xs_g{h}", align_bytes=64) for h in range(2)]
+        for h in range(2):
+            nc.vector.tensor_copy(xs_g[h][:], xs_win[:].indirect(part(l1, h * BANK, BANK)))
+        xs5_g = keep.tile([P, O], U8, name="xs5_g", align_bytes=64)
+        nc.vector.tensor_copy(xs5_g[:], xs_win[:].indirect(l5[:]))
+
+        wc_pl = [keep.tile([P, 2, R], BF16, name=f"wc_pl{e}", align_bytes=64) for e in range(2)]
+        wc_in = keep.tile([P, PACK, P, PACK], BF16, name="wc_in", align_bytes=64)
+
+        def weave(e, m0, m1):
+            nc.vector.tensor_copy(
+                wc_in[:, :, m0:m1, 2 * e : 2 * e + 2],
+                wc_pl[e][:].rearrange("p e (m c) -> p c m e", c=PACK)[:, :, m0:m1, :],
+            )
+
+        for t in range(3):
+            nc.scalar.activation(wc_pl[t // 2][:, t % 2, :], ua_win[t][:].indirect(l2[:]), COPY, scale=ha_t[:, t : t + 1])
+            if t == 1:
+                weave(0, 0, P)
+        for h in range(2):
+            nc.scalar.activation(
+                wc_pl[1][:, 1, h * 256 : (h + 1) * 256], ua_win[3][:].indirect(part(l2, h * 256, 256)), COPY, scale=ha_t[:, 3:4]
+            )
+            weave(1, h * 64, (h + 1) * 64)
+        wc_w = keep.tile([P, R], U32, name="wc_w", align_bytes=64)
+        wc_s = keep.tile([P, R], U8, name="wc_s", align_bytes=64)
+        nc.vector.quantize_mx(wc_w[:].bitcast(FP8X4), wc_s[:], wc_in[:].rearrange("p c m t -> p (c m t)"))
+
+        xw_g = [keep.tile([P, BANK], U32, name=f"xw_g{h}", align_bytes=64) for h in range(2)]
+        for h in range(2):
+            nc.vector.tensor_copy(xw_g[h][:], xw_win[:].indirect(part(l1, h * BANK, BANK)))
+
+        a_win = [keep.tile([P, J], F32, name=f"a_win{c}") for c in range(PACK)]
+
+        def first_product(c, h, engine):
+            bank = psum.tile([P, BANK], F32, name=f"bank{2 * c + h}")
+            cols = slice(c * P, (c + 1) * P)
+            nc.tensor.matmul_mx(
+                bank[:], lhsT=wc_w[:, cols].bitcast(FP8X4), lhsT_scale=wc_s[:, cols],
+                rhs=xw_g[h][:].bitcast(FP8X4), rhs_scale=xs_g[h][:], start=True, stop=True,
+            )
+            dst = a_win[c][:, h * BANK : (h + 1) * BANK]
+            if engine is nc.scalar:
+                nc.scalar.copy(dst, bank[:])
+            else:
+                nc.vector.tensor_copy(dst, bank[:])
+
+        first_product(0, 0, nc.scalar)
+        first_product(1, 0, nc.scalar)
+        first_product(0, 1, nc.vector)
+        first_product(1, 1, nc.vector)
+        for c in (2, 3):
+            for h in range(2):
+                first_product(c, h, nc.vector)
+
+        xw5_g = keep.tile([P, O], U32, name="xw5_g", align_bytes=64)
+        nc.vector.tensor_copy(xw5_g[:], xw_win[:].indirect(l5[:]))
+
+        hid = [keep.tile([P, HALF_O, PACK], BF16, name=f"hid{h}", align_bytes=64) for h in range(2)]
+        hid_w = [keep.tile([P, HALF_O], U32, name=f"hid_w{h}", align_bytes=64) for h in range(2)]
+        hid_s = [keep.tile([P, HALF_O], U8, name=f"hid_s{h}", align_bytes=64) for h in range(2)]
+        p_win = [keep.tile([P, O], F32, name=f"p_win{u}") for u in range(2)]
+
+        def pool(picked, c, h):
+            nc.vector.tensor_reduce(hid[h][:, :, c], picked.rearrange("p l (o s) -> p o l s", s=2), XY, MAX)
+
+        def second_product(h):
+            nc.vector.quantize_mx(hid_w[h][:].bitcast(FP8X4), hid_s[h][:], hid[h][:].rearrange("p o t -> p (o t)"))
+            o_cols = slice(h * HALF_O, (h + 1) * HALF_O)
+            for u in range(2):
+                bank = psum.tile([P, HALF_O], F32, name=f"bank{2 * h + u}")
+                n_cols = slice(u * P, (u + 1) * P)
+                n_bytes = slice(2 * u * P, 2 * (u + 1) * P)
+                nc.tensor.matmul_mx(
+                    bank[:], lhsT=ws_w[:, n_bytes].bitcast(FP4X4), lhsT_scale=ws_s[:, n_cols],
+                    rhs=xw5_g[:, o_cols].bitcast(FP8X4), rhs_scale=xs5_g[:, o_cols], start=True, stop=False,
+                )
+                nc.tensor.matmul_mx(
+                    bank[:], lhsT=wb_w[:, n_bytes].bitcast(FP4X4), lhsT_scale=wb_s[:, n_cols],
+                    rhs=hid_w[h][:].bitcast(FP8X4), rhs_scale=hid_s[h][:], start=False, stop=True,
+                )
+                nc.vector.tensor_copy(p_win[u][:, o_cols], bank[:])
+
+        for c in range(3):
+            picked = keep.tile([P, 2, S], F32, name=f"picked{c}")
+            nc.scalar.activation(picked[:, 0, :], a_win[c][:].indirect(l3[:]), COPY, scale=sa_t[:, c : c + 1])
+            nc.scalar.activation(picked[:, 1, :], a_win[c][:].indirect(l4[:]), COPY, scale=sb_t[:, c : c + 1])
+            for h in range(2):
+                pool(picked[:, :, h * O : (h + 1) * O], c, h)
+        for h in range(2):
+            picked = keep.tile([P, 2, O], F32, name=f"picked3{h}")
+            nc.scalar.activation(picked[:, 0, :], a_win[3][:].indirect(part(l3, h * O, O)), COPY, scale=sa_t[:, 3:4])
+            nc.scalar.activation(picked[:, 1, :], a_win[3][:].indirect(part(l4, h * O, O)), COPY, scale=sb_t[:, 3:4])
+            pool(picked[:], 3, h)
+            second_product(h)
+
+        for u in range(2):
+            pair = keep.tile([P, 2, U], F32, name=f"pair{u}")
+            nc.scalar.activation(pair[:, 0, :], p_win[u][:].indirect(l6[:]), COPY, scale=so_t[:, u : u + 1])
+            nc.scalar.activation(pair[:, 1, :], p_win[u][:].indirect(l7[:]), COPY, scale=sp_t[:, u : u + 1])
+            res = keep.tile([P, U], F32, name=f"res{u}")
+            nc.vector.tensor_tensor(res[:], pair[:, 0, :], pair[:, 1, :], MAX)
+            nc.sync.dma_start(out[u * P : (u + 1) * P, :], res[:])

@@ -45,35 +45,42 @@ def tile_picked_tokens_codes_one_pooledgroups_further_grouppairs_kernel(
         def part(lst, start, n):
             return lst[:, start // PER_COL : (start + n) // PER_COL]
 
-        xs_win = keep.tile([P, T], U8, name="xs_win", align_bytes=64)
-        nc.vector.memset(xs_win[:].bitcast(I32), 0)
+        ha_t = keep.tile([P, PACK], F32, name="ha_t")
+        nc.scalar.dma_start(ha_t[:], ha.rearrange("(p t) o -> p (t o)", t=PACK))
+        warm = keep.tile([P, 2], F32, name="warm")
+        nc.gpsimd.memset(warm[:, 0:1], 0.0)
+        nc.scalar.activation(warm[:, 1:2], warm[:, 0:1], COPY)
         ua_rows = ua.rearrange("(p t) f -> t p f", t=PACK)
         ua_win = [keep.tile([P, F], F32, name=f"ua_win{t}") for t in range(PACK)]
         l2 = load_list(offs2, "l2")
+        nc.sync.dma_start(ua_win[0][:], ua_rows[0])
+        xs_stage = keep.tile([P, 2, T // 4], I32, name="xs_stage")
+        xs_rows = xt_scales[0].bitcast(I32).rearrange("(e q i) c -> e i q c", q=2, i=4)
+        for e in range(2):
+            nc.sync.dma_start(xs_stage[64 * e : 64 * e + 4, :, :], xs_rows[e])
         l1 = load_list(offs, "l1")
-        nc.scalar.dma_start(ua_win[0][:], ua_rows[0])
-        nc.scalar.dma_start(ua_win[1][:], ua_rows[1])
-        ha_t = keep.tile([P, PACK], F32, name="ha_t")
-        nc.gpsimd.dma_start(ha_t[:], ha.rearrange("(p t) o -> p (t o)", t=PACK))
-        load_scale_rows(xs_win, xt_scales, nc.sync)
-        nc.sync.dma_start(ua_win[2][:], ua_rows[2])
-        nc.sync.dma_start(ua_win[3][:], ua_rows[3])
-        l5 = load_list(offs5, "l5")
+        for t in range(1, PACK):
+            nc.sync.dma_start(ua_win[t][:], ua_rows[t])
         xw_win = keep.tile([P, T], U32, name="xw_win", align_bytes=64)
         nc.sync.dma_start(xw_win[:].bitcast(I32), xt_words[0].rearrange("p n t -> p (n t)").bitcast(I32))
+        xs_win = keep.tile([P, T], U8, name="xs_win", align_bytes=64)
+        nc.vector.memset(xs_win[:].bitcast(I32), 0)
+        for q in range(4):
+            nc.vector.tensor_copy(xs_win[32 * q : 32 * q + 4, :].bitcast(I32), xs_stage[64 * (q // 2) : 64 * (q // 2) + 4, q % 2, :])
         l3 = load_list(offs3, "l3")
-        l4 = load_list(offs4, "l4")
         sa_t = keep.tile([P, PACK], F32, name="sa_t")
         nc.sync.dma_start(sa_t[:], sa.rearrange("(p t) o -> p (t o)", t=PACK))
+        l4 = load_list(offs4, "l4")
         sb_t = keep.tile([P, PACK], F32, name="sb_t")
         nc.sync.dma_start(sb_t[:], sb.rearrange("(p t) o -> p (t o)", t=PACK))
 
+        l5 = load_list(offs5, "l5")
         ws_w = keep.tile([P, 2 * N], U8, name="ws_w", align_bytes=64)
         wb_w = keep.tile([P, 2 * N], U8, name="wb_w", align_bytes=64)
         ws_s = keep.tile([P, N], U8, name="ws_s", align_bytes=64)
         wb_s = keep.tile([P, N], U8, name="wb_s", align_bytes=64)
-        nc.gpsimd.memset(ws_s[:].bitcast(I32), 0)
-        nc.gpsimd.memset(wb_s[:].bitcast(I32), 0)
+        nc.vector.memset(ws_s[:].bitcast(I32), 0)
+        nc.vector.memset(wb_s[:].bitcast(I32), 0)
         nc.sync.dma_start(ws_w[:].bitcast(I32), ws_words[0].bitcast(I32))
         load_scale_rows(ws_s, ws_scales, nc.sync)
         nc.sync.dma_start(wb_w[:].bitcast(I32), wb_words[0].bitcast(I32))
@@ -89,59 +96,65 @@ def tile_picked_tokens_codes_one_pooledgroups_further_grouppairs_kernel(
         xs_g = [keep.tile([P, BANK], U8, name=f"xs_g{h}", align_bytes=64) for h in range(2)]
         for h in range(2):
             nc.vector.tensor_copy(xs_g[h][:], xs_win[:].indirect(part(l1, h * BANK, BANK)))
-        xs5_g = keep.tile([P, O], U8, name="xs5_g", align_bytes=64)
-        nc.vector.tensor_copy(xs5_g[:], xs_win[:].indirect(l5[:]))
 
-        wc_pl = [keep.tile([P, 2, R], BF16, name=f"wc_pl{e}", align_bytes=64) for e in range(2)]
-        wc_in = keep.tile([P, PACK, P, PACK], BF16, name="wc_in", align_bytes=64)
-
-        def weave(e, m0, m1):
-            nc.vector.tensor_copy(
-                wc_in[:, :, m0:m1, 2 * e : 2 * e + 2],
-                wc_pl[e][:].rearrange("p e (m c) -> p c m e", c=PACK)[:, :, m0:m1, :],
-            )
-
-        for t in range(3):
-            nc.scalar.activation(wc_pl[t // 2][:, t % 2, :], ua_win[t][:].indirect(l2[:]), COPY, scale=ha_t[:, t : t + 1])
-            if t == 1:
-                weave(0, 0, P)
-        for h in range(2):
-            nc.scalar.activation(
-                wc_pl[1][:, 1, h * 256 : (h + 1) * 256], ua_win[3][:].indirect(part(l2, h * 256, 256)), COPY, scale=ha_t[:, 3:4]
-            )
-            weave(1, h * 64, (h + 1) * 64)
-        wc_w = keep.tile([P, R], U32, name="wc_w", align_bytes=64)
-        wc_s = keep.tile([P, R], U8, name="wc_s", align_bytes=64)
-        nc.vector.quantize_mx(wc_w[:].bitcast(FP8X4), wc_s[:], wc_in[:].rearrange("p c m t -> p (c m t)"))
+        wc_pl = keep.tile([P, PACK, R], BF16, name="wc_pl", align_bytes=64)
+        for t in range(PACK):
+            nc.scalar.activation(wc_pl[:, t, :], ua_win[t][:].indirect(l2[:]), COPY, scale=ha_t[:, t : t + 1])
+        by_class = wc_pl[:].rearrange("p t (m c) -> p m t c", c=PACK)
+        wc_in0 = keep.tile([P, P, PACK], BF16, name="wc_in0", tag="xw_g0", align_bytes=64)
+        wc_in1 = keep.tile([P, 2, P, PACK], BF16, name="wc_in1", align_bytes=64)
+        nc.vector.tensor_copy(wc_in0[:, :, 0:3], by_class[:, :, 0:3, 0])
+        nc.vector.tensor_copy(wc_in0[:, :, 3], by_class[:, :, 3, 0])
+        nc.scalar.copy(
+            wc_in1[:].rearrange("p c (a b) t -> p a c b t", b=2),
+            wc_pl[:].rearrange("p t (a b c) -> p a c b t", b=2, c=PACK)[:, :, 1:3, :, :],
+        )
+        wc_w0 = keep.tile([P, P], U32, name="wc_w0", align_bytes=64)
+        wc_s0 = keep.tile([P, P], U8, name="wc_s0", align_bytes=64)
+        nc.vector.quantize_mx(wc_w0[:].bitcast(FP8X4), wc_s0[:], wc_in0[:].rearrange("p m t -> p (m t)"))
+        wc_w = [wc_w0[:]]
+        wc_s = [wc_s0[:]]
 
         xw_g = [keep.tile([P, BANK], U32, name=f"xw_g{h}", align_bytes=64) for h in range(2)]
-        for h in range(2):
-            nc.vector.tensor_copy(xw_g[h][:], xw_win[:].indirect(part(l1, h * BANK, BANK)))
+        pieces = [(0, 512), (512, 256), (768, 128), (896, 128)]
+        for j0, n in pieces:
+            h, j = divmod(j0, BANK)
+            nc.vector.tensor_copy(xw_g[h][:, j : j + n], xw_win[:].indirect(part(l1, j0, n)))
 
         a_win = [keep.tile([P, J], F32, name=f"a_win{c}") for c in range(PACK)]
 
-        def first_product(c, h, engine):
-            bank = psum.tile([P, BANK], F32, name=f"bank{2 * c + h}")
-            cols = slice(c * P, (c + 1) * P)
+        def first_product(c, j0, n, bank_no, engine):
+            bank = psum.tile([P, n], F32, name=f"bank{bank_no}")
+            h, j = divmod(j0, BANK)
             nc.tensor.matmul_mx(
-                bank[:], lhsT=wc_w[:, cols].bitcast(FP8X4), lhsT_scale=wc_s[:, cols],
-                rhs=xw_g[h][:].bitcast(FP8X4), rhs_scale=xs_g[h][:], start=True, stop=True,
+                bank[:], lhsT=wc_w[c].bitcast(FP8X4), lhsT_scale=wc_s[c],
+                rhs=xw_g[h][:, j : j + n].bitcast(FP8X4), rhs_scale=xs_g[h][:, j : j + n], start=True, stop=True,
             )
-            dst = a_win[c][:, h * BANK : (h + 1) * BANK]
+            dst = a_win[c][:, j0 : j0 + n]
             if engine is nc.scalar:
                 nc.scalar.copy(dst, bank[:])
             else:
                 nc.vector.tensor_copy(dst, bank[:])
 
-        first_product(0, 0, nc.scalar)
-        first_product(1, 0, nc.scalar)
-        first_product(0, 1, nc.vector)
-        first_product(1, 1, nc.vector)
-        for c in (2, 3):
+        for i, (j0, n) in enumerate(pieces):
+            first_product(0, j0, n, i, nc.scalar)
+        wc_w1 = keep.tile([P, R - P], U32, name="wc_w1", tag="wc_w0", align_bytes=64)
+        wc_s1 = keep.tile([P, R - P], U8, name="wc_s1", align_bytes=64)
+        wc_in3 = keep.tile([P, P, PACK], BF16, name="wc_in3", tag="wc_s0", align_bytes=64)
+        for c, src in enumerate((wc_in1[:, 0, :, :], wc_in1[:, 1, :, :], wc_in3[:])):
+            cols = slice(c * P, (c + 1) * P)
+            if c == 2:
+                nc.vector.tensor_copy(wc_in3[:], by_class[:, :, :, 3])
+            nc.vector.quantize_mx(wc_w1[:, cols].bitcast(FP8X4), wc_s1[:, cols], src.rearrange("p m t -> p (m t)"))
+        wc_w.extend([wc_w1[:, c * P : (c + 1) * P] for c in range(PACK - 1)])
+        wc_s.extend([wc_s1[:, c * P : (c + 1) * P] for c in range(PACK - 1)])
+        for c in range(1, PACK):
             for h in range(2):
-                first_product(c, h, nc.vector)
+                first_product(c, h * BANK, BANK, (2 + 2 * c + h) % 8, nc.vector)
 
-        xw5_g = keep.tile([P, O], U32, name="xw5_g", align_bytes=64)
+        xs5_g = keep.tile([P, O], U8, name="xs5_g", tag="xs_g0", align_bytes=64)
+        nc.vector.tensor_copy(xs5_g[:], xs_win[:].indirect(l5[:]))
+        xw5_g = keep.tile([P, O], U32, name="xw5_g", tag="xw_g0", align_bytes=64)
         nc.vector.tensor_copy(xw5_g[:], xw_win[:].indirect(l5[:]))
 
         hid = [keep.tile([P, HALF_O, PACK], BF16, name=f"hid{h}", align_bytes=64) for h in range(2)]
@@ -149,14 +162,30 @@ def tile_picked_tokens_codes_one_pooledgroups_further_grouppairs_kernel(
         hid_s = [keep.tile([P, HALF_O], U8, name=f"hid_s{h}", align_bytes=64) for h in range(2)]
         p_win = [keep.tile([P, O], F32, name=f"p_win{u}") for u in range(2)]
 
-        def pool(picked, c, h):
-            nc.vector.tensor_reduce(hid[h][:, :, c], picked.rearrange("p l (o s) -> p o l s", s=2), XY, MAX)
+        planes = keep.tile([P, PACK, O], BF16, name="planes", align_bytes=64)
+
+        def pick(c, s0, n):
+            picked = keep.tile([P, 2, n], F32, name=f"picked{c}_{s0}")
+            nc.scalar.activation(picked[:, 0, :], a_win[c][:].indirect(part(l3, s0, n)), COPY, scale=sa_t[:, c : c + 1])
+            nc.scalar.activation(picked[:, 1, :], a_win[c][:].indirect(part(l4, s0, n)), COPY, scale=sb_t[:, c : c + 1])
+            return picked
+
+        def pool_to_plane(picked, c, s0, n):
+            h1 = keep.tile([P, n], F32, name=f"h1_{c}")
+            nc.vector.tensor_tensor(h1[:], picked[:, 0, :], picked[:, 1, :], MAX)
+            nc.vector.tensor_tensor(planes[:, c, s0 // 2 : (s0 + n) // 2], h1[:, 0:n:2], h1[:, 1:n:2], MAX)
+
+        def pool_in_place(picked, c, o0, o1):
+            nc.vector.tensor_reduce(
+                hid[1][:, o0:o1, c], picked[:, :, 2 * o0 : 2 * o1].rearrange("p l (o s) -> p o l s", s=2), XY, MAX
+            )
 
         def second_product(h):
+            banks = []
             nc.vector.quantize_mx(hid_w[h][:].bitcast(FP8X4), hid_s[h][:], hid[h][:].rearrange("p o t -> p (o t)"))
             o_cols = slice(h * HALF_O, (h + 1) * HALF_O)
             for u in range(2):
-                bank = psum.tile([P, HALF_O], F32, name=f"bank{2 * h + u}")
+                bank = psum.tile([P, HALF_O], F32, name=f"bank{2 + 2 * h + u}")
                 n_cols = slice(u * P, (u + 1) * P)
                 n_bytes = slice(2 * u * P, 2 * (u + 1) * P)
                 nc.tensor.matmul_mx(
@@ -167,20 +196,29 @@ def tile_picked_tokens_codes_one_pooledgroups_further_grouppairs_kernel(
                     bank[:], lhsT=wb_w[:, n_bytes].bitcast(FP4X4), lhsT_scale=wb_s[:, n_cols],
                     rhs=hid_w[h][:].bitcast(FP8X4), rhs_scale=hid_s[h][:], start=False, stop=True,
                 )
-                nc.vector.tensor_copy(p_win[u][:, o_cols], bank[:])
+                banks.append((p_win[u][:, o_cols], bank))
+            return banks
 
-        for c in range(3):
-            picked = keep.tile([P, 2, S], F32, name=f"picked{c}")
-            nc.scalar.activation(picked[:, 0, :], a_win[c][:].indirect(l3[:]), COPY, scale=sa_t[:, c : c + 1])
-            nc.scalar.activation(picked[:, 1, :], a_win[c][:].indirect(l4[:]), COPY, scale=sb_t[:, c : c + 1])
-            for h in range(2):
-                pool(picked[:, :, h * O : (h + 1) * O], c, h)
-        for h in range(2):
-            picked = keep.tile([P, 2, O], F32, name=f"picked3{h}")
-            nc.scalar.activation(picked[:, 0, :], a_win[3][:].indirect(part(l3, h * O, O)), COPY, scale=sa_t[:, 3:4])
-            nc.scalar.activation(picked[:, 1, :], a_win[3][:].indirect(part(l4, h * O, O)), COPY, scale=sb_t[:, 3:4])
-            pool(picked[:], 3, h)
-            second_product(h)
+        for c in range(2):
+            pool_to_plane(pick(c, 0, S), c, 0, S)
+        nc.vector.tensor_copy(hid[1][:, :, 0:2], planes[:, 0:2, HALF_O:O].rearrange("p c o -> p o c"))
+        for c in (2, 3):
+            pool_to_plane(pick(c, 0, O), c, 0, O)
+        nc.vector.tensor_copy(hid[0][:], planes[:, :, 0:HALF_O].rearrange("p c o -> p o c"))
+        first_half = second_product(0)
+        pool_in_place(pick(2, O, O), 2, 0, HALF_O)
+        last = keep.tile([P, 2, O], F32, name="last")
+        nc.scalar.activation(last[:, 0, :], a_win[3][:].indirect(part(l3, O, O)), COPY, scale=sa_t[:, 3:4])
+        for i in range(2):
+            nc.scalar.activation(
+                last[:, 1, i * P : (i + 1) * P], a_win[3][:].indirect(part(l4, O + i * P, P)), COPY, scale=sb_t[:, 3:4]
+            )
+            pool_in_place(last, 3, i * P // 2, (i + 1) * P // 2)
+        for dst, bank in first_half:
+            nc.scalar.copy(dst, bank[:])
+        second_half = second_product(1)
+        nc.scalar.copy(second_half[0][0], second_half[0][1][:])
+        nc.vector.tensor_copy(second_half[1][0], second_half[1][1][:])
 
         for u in range(2):
             pair = keep.tile([P, 2, U], F32, name=f"pair{u}")

from contextlib import ExitStack

import concourse.mybir as mybir

K, J, R, T, F, S, O, N, U = 512, 1024, 512, 2048, 1024, 512, 256, 256, 128
FLOPS = 2 * K * R * J + 2 * R * N * O + 2 * K * N * O

F32 = mybir.dt.float32
BF16 = mybir.dt.bfloat16
I32 = mybir.dt.int32
U32 = mybir.dt.uint32
U16 = mybir.dt.uint16
U8 = mybir.dt.uint8
FP8X4 = mybir.dt.float8_e4m3fn_x4
FP4X4 = mybir.dt.float4_e2m1fn_x4
COPY = mybir.ActivationFunctionType.Copy
MAX = mybir.AluOpType.max
XY = mybir.AxisListType.XY

P = 128
PACK = 4
PER_COL = 16
BANK = 512
HALF_O = O // 2


def tile_picked_tokens_codes_one_pooledgroups_further_grouppairs_kernel(
    tc, xt_words, xt_scales, ua, ha, sa, sb, wb_words, wb_scales, ws_words, ws_scales, so, sp,
    offs, offs2, offs3, offs4, offs5, offs6, offs7, out,
):
    nc = tc.nc
    with ExitStack() as ctx:
        keep = ctx.enter_context(tc.tile_pool(name="keep", bufs=1))
        psum = ctx.enter_context(tc.psum_pool(name="psum", bufs=1))

        def load_list(src, name):
            t = keep.tile(list(src.shape), U16, name=name)
            nc.sync.dma_start(t[:], src)
            return t

        def load_scale_rows(dst, src, queue):
            for q in range(4):
                queue.dma_start(dst[32 * q : 32 * q + 4, :].bitcast(I32), src[0, 4 * q : 4 * q + 4, :].bitcast(I32))

        def part(lst, start, n):
            return lst[:, start // PER_COL : (start + n) // PER_COL]

        ha_t = keep.tile([P, PACK], F32, name="ha_t")
        nc.scalar.dma_start(ha_t[:], ha.rearrange("(p t) o -> p (t o)", t=PACK))
        warm = keep.tile([P, 2], F32, name="warm")
        nc.gpsimd.memset(warm[:, 0:1], 0.0)
        nc.scalar.activation(warm[:, 1:2], warm[:, 0:1], COPY)
        ua_rows = ua.rearrange("(p t) f -> t p f", t=PACK)
        ua_win = [keep.tile([P, F], F32, name=f"ua_win{t}") for t in range(PACK)]
        l2 = load_list(offs2, "l2")
        nc.sync.dma_start(ua_win[0][:], ua_rows[0])
        xs_stage = keep.tile([P, 2, T // 4], I32, name="xs_stage")
        xs_rows = xt_scales[0].bitcast(I32).rearrange("(e q i) c -> e i q c", q=2, i=4)
        for e in range(2):
            nc.sync.dma_start(xs_stage[64 * e : 64 * e + 4, :, :], xs_rows[e])
        l1 = load_list(offs, "l1")
        for t in range(1, PACK):
            nc.sync.dma_start(ua_win[t][:], ua_rows[t])
        xw_win = keep.tile([P, T], U32, name="xw_win", align_bytes=64)
        nc.sync.dma_start(xw_win[:].bitcast(I32), xt_words[0].rearrange("p n t -> p (n t)").bitcast(I32))
        xs_win = keep.tile([P, T], U8, name="xs_win", align_bytes=64)
        nc.vector.memset(xs_win[:].bitcast(I32), 0)
        for q in range(4):
            nc.vector.tensor_copy(xs_win[32 * q : 32 * q + 4, :].bitcast(I32), xs_stage[64 * (q // 2) : 64 * (q // 2) + 4, q % 2, :])
        l3 = load_list(offs3, "l3")
        sa_t = keep.tile([P, PACK], F32, name="sa_t")
        nc.sync.dma_start(sa_t[:], sa.rearrange("(p t) o -> p (t o)", t=PACK))
        l4 = load_list(offs4, "l4")
        sb_t = keep.tile([P, PACK], F32, name="sb_t")
        nc.sync.dma_start(sb_t[:], sb.rearrange("(p t) o -> p (t o)", t=PACK))

        l5 = load_list(offs5, "l5")
        ws_w = keep.tile([P, 2 * N], U8, name="ws_w", align_bytes=64)
        wb_w = keep.tile([P, 2 * N], U8, name="wb_w", align_bytes=64)
        ws_s = keep.tile([P, N], U8, name="ws_s", align_bytes=64)
        wb_s = keep.tile([P, N], U8, name="wb_s", align_bytes=64)
        nc.vector.memset(ws_s[:].bitcast(I32), 0)
        nc.vector.memset(wb_s[:].bitcast(I32), 0)
        nc.sync.dma_start(ws_w[:].bitcast(I32), ws_words[0].bitcast(I32))
        load_scale_rows(ws_s, ws_scales, nc.sync)
        nc.sync.dma_start(wb_w[:].bitcast(I32), wb_words[0].bitcast(I32))
        load_scale_rows(wb_s, wb_scales, nc.sync)
        l6 = load_list(offs6, "l6")
        l7 = load_list(offs7, "l7")
        so_t = keep.tile([P, 2], F32, name="so_t")
        sp_t = keep.tile([P, 2], F32, name="sp_t")
        with nc.allow_non_contiguous_dma(reason="one value a partition and output tile"):
            nc.sync.dma_start(so_t[:], so.rearrange("(u p) o -> p (u o)", p=P))
            nc.sync.dma_start(sp_t[:], sp.rearrange("(u p) o -> p (u o)", p=P))

        xs_g = [keep.tile([P, BANK], U8, name=f"xs_g{h}", align_bytes=64) for h in range(2)]
        for h in range(2):
            nc.vector.tensor_copy(xs_g[h][:], xs_win[:].indirect(part(l1, h * BANK, BANK)))

        wc_pl = keep.tile([P, PACK, R], BF16, name="wc_pl", align_bytes=64)
        for t in range(PACK):
            nc.scalar.activation(wc_pl[:, t, :], ua_win[t][:].indirect(l2[:]), COPY, scale=ha_t[:, t : t + 1])
        by_class = wc_pl[:].rearrange("p t (m c) -> p m t c", c=PACK)
        wc_in0 = keep.tile([P, P, PACK], BF16, name="wc_in0", tag="xw_g0", align_bytes=64)
        wc_in1 = keep.tile([P, 2, P, PACK], BF16, name="wc_in1", align_bytes=64)
        nc.vector.tensor_copy(wc_in0[:, :, 0:3], by_class[:, :, 0:3, 0])
        nc.vector.tensor_copy(wc_in0[:, :, 3], by_class[:, :, 3, 0])
        nc.scalar.copy(
            wc_in1[:].rearrange("p c (a b) t -> p a c b t", b=2),
            wc_pl[:].rearrange("p t (a b c) -> p a c b t", b=2, c=PACK)[:, :, 1:3, :, :],
        )
        wc_w0 = keep.tile([P, P], U32, name="wc_w0", align_bytes=64)
        wc_s0 = keep.tile([P, P], U8, name="wc_s0", align_bytes=64)
        nc.vector.quantize_mx(wc_w0[:].bitcast(FP8X4), wc_s0[:], wc_in0[:].rearrange("p m t -> p (m t)"))
        wc_w = [wc_w0[:]]
        wc_s = [wc_s0[:]]

        xw_g = [keep.tile([P, BANK], U32, name=f"xw_g{h}", align_bytes=64) for h in range(2)]
        pieces = [(0, 512), (512, 256), (768, 128), (896, 128)]
        for j0, n in pieces:
            h, j = divmod(j0, BANK)
            nc.vector.tensor_copy(xw_g[h][:, j : j + n], xw_win[:].indirect(part(l1, j0, n)))

        a_win = [keep.tile([P, J], F32, name=f"a_win{c}") for c in range(PACK)]

        def first_product(c, j0, n, bank_no, engine):
            bank = psum.tile([P, n], F32, name=f"bank{bank_no}")
            h, j = divmod(j0, BANK)
            nc.tensor.matmul_mx(
                bank[:], lhsT=wc_w[c].bitcast(FP8X4), lhsT_scale=wc_s[c],
                rhs=xw_g[h][:, j : j + n].bitcast(FP8X4), rhs_scale=xs_g[h][:, j : j + n], start=True, stop=True,
            )
            dst = a_win[c][:, j0 : j0 + n]
            if engine is nc.scalar:
                nc.scalar.copy(dst, bank[:])
            else:
                nc.vector.tensor_copy(dst, bank[:])

        for i, (j0, n) in enumerate(pieces):
            first_product(0, j0, n, i, nc.scalar)
        wc_w1 = keep.tile([P, R - P], U32, name="wc_w1", tag="wc_w0", align_bytes=64)
        wc_s1 = keep.tile([P, R - P], U8, name="wc_s1", align_bytes=64)
        wc_in3 = keep.tile([P, P, PACK], BF16, name="wc_in3", tag="wc_s0", align_bytes=64)
        for c, src in enumerate((wc_in1[:, 0, :, :], wc_in1[:, 1, :, :], wc_in3[:])):
            cols = slice(c * P, (c + 1) * P)
            if c == 2:
                nc.vector.tensor_copy(wc_in3[:], by_class[:, :, :, 3])
            nc.vector.quantize_mx(wc_w1[:, cols].bitcast(FP8X4), wc_s1[:, cols], src.rearrange("p m t -> p (m t)"))
        wc_w.extend([wc_w1[:, c * P : (c + 1) * P] for c in range(PACK - 1)])
        wc_s.extend([wc_s1[:, c * P : (c + 1) * P] for c in range(PACK - 1)])
        for c in range(1, PACK):
            for h in range(2):
                first_product(c, h * BANK, BANK, (2 + 2 * c + h) % 8, nc.vector)

        xs5_g = keep.tile([P, O], U8, name="xs5_g", tag="xs_g0", align_bytes=64)
        nc.vector.tensor_copy(xs5_g[:], xs_win[:].indirect(l5[:]))
        xw5_g = keep.tile([P, O], U32, name="xw5_g", tag="xw_g0", align_bytes=64)
        nc.vector.tensor_copy(xw5_g[:], xw_win[:].indirect(l5[:]))

        hid = [keep.tile([P, HALF_O, PACK], BF16, name=f"hid{h}", align_bytes=64) for h in range(2)]
        hid_w = [keep.tile([P, HALF_O], U32, name=f"hid_w{h}", align_bytes=64) for h in range(2)]
        hid_s = [keep.tile([P, HALF_O], U8, name=f"hid_s{h}", align_bytes=64) for h in range(2)]
        p_win = [keep.tile([P, O], F32, name=f"p_win{u}") for u in range(2)]

        planes = keep.tile([P, PACK, O], BF16, name="planes", align_bytes=64)

        def pick(c, s0, n):
            picked = keep.tile([P, 2, n], F32, name=f"picked{c}_{s0}")
            nc.scalar.activation(picked[:, 0, :], a_win[c][:].indirect(part(l3, s0, n)), COPY, scale=sa_t[:, c : c + 1])
            nc.scalar.activation(picked[:, 1, :], a_win[c][:].indirect(part(l4, s0, n)), COPY, scale=sb_t[:, c : c + 1])
            return picked

        def pool_to_plane(picked, c, s0, n):
            h1 = keep.tile([P, n], F32, name=f"h1_{c}")
            nc.vector.tensor_tensor(h1[:], picked[:, 0, :], picked[:, 1, :], MAX)
            nc.vector.tensor_tensor(planes[:, c, s0 // 2 : (s0 + n) // 2], h1[:, 0:n:2], h1[:, 1:n:2], MAX)

        def pool_in_place(picked, c, o0, o1):
            nc.vector.tensor_reduce(
                hid[1][:, o0:o1, c], picked[:, :, 2 * o0 : 2 * o1].rearrange("p l (o s) -> p o l s", s=2), XY, MAX
            )

        def second_product(h):
            banks = []
            nc.vector.quantize_mx(hid_w[h][:].bitcast(FP8X4), hid_s[h][:], hid[h][:].rearrange("p o t -> p (o t)"))
            o_cols = slice(h * HALF_O, (h + 1) * HALF_O)
            for u in range(2):
                bank = psum.tile([P, HALF_O], F32, name=f"bank{2 + 2 * h + u}")
                n_cols = slice(u * P, (u + 1) * P)
                n_bytes = slice(2 * u * P, 2 * (u + 1) * P)
                nc.tensor.matmul_mx(
                    bank[:], lhsT=ws_w[:, n_bytes].bitcast(FP4X4), lhsT_scale=ws_s[:, n_cols],
                    rhs=xw5_g[:, o_cols].bitcast(FP8X4), rhs_scale=xs5_g[:, o_cols], start=True, stop=False,
                )
                nc.tensor.matmul_mx(
                    bank[:], lhsT=wb_w[:, n_bytes].bitcast(FP4X4), lhsT_scale=wb_s[:, n_cols],
                    rhs=hid_w[h][:].bitcast(FP8X4), rhs_scale=hid_s[h][:], start=False, stop=True,
                )
                banks.append((p_win[u][:, o_cols], bank))
            return banks

        for c in range(2):
            pool_to_plane(pick(c, 0, S), c, 0, S)
        nc.vector.tensor_copy(hid[1][:, :, 0:2], planes[:, 0:2, HALF_O:O].rearrange("p c o -> p o c"))
        for c in (2, 3):
            pool_to_plane(pick(c, 0, O), c, 0, O)
        nc.vector.tensor_copy(hid[0][:], planes[:, :, 0:HALF_O].rearrange("p c o -> p o c"))
        first_half = second_product(0)
        pool_in_place(pick(2, O, O), 2, 0, HALF_O)
        last = keep.tile([P, 2, O], F32, name="last")
        nc.scalar.activation(last[:, 0, :], a_win[3][:].indirect(part(l3, O, O)), COPY, scale=sa_t[:, 3:4])
        for i in range(2):
            nc.scalar.activation(
                last[:, 1, i * P : (i + 1) * P], a_win[3][:].indirect(part(l4, O + i * P, P)), COPY, scale=sb_t[:, 3:4]
            )
            pool_in_place(last, 3, i * P // 2, (i + 1) * P // 2)
        for dst, bank in first_half:
            nc.scalar.copy(dst, bank[:])
        second_half = second_product(1)
        nc.scalar.copy(second_half[0][0], second_half[0][1][:])
        nc.vector.tensor_copy(second_half[1][0], second_half[1][1][:])

        for u in range(2):
            pair = keep.tile([P, 2, U], F32, name=f"pair{u}")
            nc.scalar.activation(pair[:, 0, :], p_win[u][:].indirect(l6[:]), COPY, scale=so_t[:, u : u + 1])
            nc.scalar.activation(pair[:, 1, :], p_win[u][:].indirect(l7[:]), COPY, scale=sp_t[:, u : u + 1])
            res = keep.tile([P, U], F32, name=f"res{u}")
            nc.vector.tensor_tensor(res[:], pair[:, 0, :], pair[:, 1, :], MAX)
            nc.sync.dma_start(out[u * P : (u + 1) * P, :], res[:])
